import numpy as np
import ml_dtypes

BF16 = ml_dtypes.bfloat16


def bf(x):
    return np.asarray(x, np.float32).astype(BF16)


def f32(x):
    return np.asarray(x, np.float32)


def f64(x):
    return np.asarray(x).astype(np.float64)


def striped(idx):
    return np.tile(idx.reshape(-1, 16).T, (8, 1))


def rows(idx, k):
    return np.tile(idx, (k, 1))


def look(tab, idx):
    return np.take_along_axis(f64(tab), rows(idx, len(tab)), axis=1)


K, S, V, N = 256, 2048, 1024, 1024


def setup_inputs():
    return {"tab": f32(np.random.standard_normal((2, K, S))), "y": f32(np.random.standard_normal((K, V))), "offs": striped(np.random.permutation(S)[:N])}


def reference(tab, y, offs):
    idx = offs[:16].T.reshape(-1)
    x = (np.minimum(look(tab[0], idx), f64(y))) * (1.0 / (1.0 + np.exp(-look(tab[1], idx))))
    return x

@@ -1,0 +1,45 @@
+import concourse.mybir as mybir
+
+P = 128
+PIECE = 256
+F32 = mybir.dt.float32
+BYTES = 4 * (2 * 256 * 2048 + 2 * 256 * 1024) + 2 * 128 * 64
+
+
+def tile_lookup_vg_minsig_out_kernel(tc, tab, y, offs, out):
+    nc = tc.nc
+    K, S = tab.shape[1], tab.shape[2]
+    N = y.shape[1]
+    BLOCKS = K // P
+    with tc.tile_pool(name="held", bufs=1) as held, tc.tile_pool(name="blocks", bufs=BLOCKS) as blocks:
+        offsets = held.tile([P, N // 16], mybir.dt.uint16)
+        nc.sync.dma_start(offsets[:], offs)
+
+        values, stream, gates = [], [], []
+        for b in range(BLOCKS):
+            rows = slice(b * P, (b + 1) * P)
+            values.append(blocks.tile([P, S], F32, name="values"))
+            nc.sync.dma_start(values[b][:], tab[0, rows, :])
+            stream.append(blocks.tile([P, N], F32, name="stream"))
+            nc.sync.dma_start(stream[b][:], y[rows, :])
+            gates.append(blocks.tile([P, S], F32, name="gates"))
+            nc.sync.dma_start(gates[b][:], tab[1, rows, :])
+
+        for b in range(BLOCKS):
+            rows = slice(b * P, (b + 1) * P)
+            least = blocks.tile([P, N], F32)
+            gate = blocks.tile([P, N], F32)
+            x = blocks.tile([P, N], F32)
+            for j in range(0, N, PIECE):
+                picked = offsets[:, j // 16 : (j + PIECE) // 16]
+                cols = slice(j, j + PIECE)
+                nc.vector.tensor_tensor(
+                    least[:, cols], values[b][:].indirect(picked), stream[b][:, cols], mybir.AluOpType.min
+                )
+                nc.scalar.activation(
+                    gate[:, cols], gates[b][:].indirect(picked), mybir.ActivationFunctionType.Sigmoid
+                )
+            for j in range(0, N, PIECE):
+                cols = slice(j, j + PIECE)
+                nc.vector.tensor_tensor(x[:, cols], least[:, cols], gate[:, cols], mybir.AluOpType.mult)
+                nc.sync.dma_start(out[rows, cols], x[:, cols])

@@ -2,6 +2,8 @@ import concourse.mybir as mybir
 
 P = 128
 PIECE = 256
+LAST_WIDTHS = (256, 256, 128, 128, 128, 128)
+LATE = 384
 F32 = mybir.dt.float32
 BYTES = 4 * (2 * 256 * 2048 + 2 * 256 * 1024) + 2 * 128 * 64
 
@@ -13,33 +15,42 @@ def tile_lookup_vg_minsig_out_kernel(tc, tab, y, offs, out):
     BLOCKS = K // P
     with tc.tile_pool(name="held", bufs=1) as held, tc.tile_pool(name="blocks", bufs=BLOCKS) as blocks:
         offsets = held.tile([P, N // 16], mybir.dt.uint16)
-        nc.sync.dma_start(offsets[:], offs)
+
+        warm_in = held.tile([P, 8], F32)
+        warm_out = held.tile([P, 8], F32)
+        nc.vector.memset(warm_in[:], 0.0)
+        nc.scalar.activation(warm_out[:], warm_in[:], mybir.ActivationFunctionType.Sigmoid)
 
         values, stream, gates = [], [], []
         for b in range(BLOCKS):
             rows = slice(b * P, (b + 1) * P)
+            early = N - LATE if b == BLOCKS - 1 else N
             values.append(blocks.tile([P, S], F32, name="values"))
             nc.sync.dma_start(values[b][:], tab[0, rows, :])
+            if b == 0:
+                nc.sync.dma_start(offsets[:], offs)
             stream.append(blocks.tile([P, N], F32, name="stream"))
-            nc.sync.dma_start(stream[b][:], y[rows, :])
+            nc.sync.dma_start(stream[b][:, :early], y[rows, :early])
             gates.append(blocks.tile([P, S], F32, name="gates"))
             nc.sync.dma_start(gates[b][:], tab[1, rows, :])
+            if early < N:
+                nc.sync.dma_start(stream[b][:, early:], y[rows, early:])
 
         for b in range(BLOCKS):
             rows = slice(b * P, (b + 1) * P)
+            widths = LAST_WIDTHS if b == BLOCKS - 1 else (PIECE,) * (N // PIECE)
+            pieces = [slice(sum(widths[:k]), sum(widths[: k + 1])) for k in range(len(widths))]
             least = blocks.tile([P, N], F32)
             gate = blocks.tile([P, N], F32)
             x = blocks.tile([P, N], F32)
-            for j in range(0, N, PIECE):
-                picked = offsets[:, j // 16 : (j + PIECE) // 16]
-                cols = slice(j, j + PIECE)
+            for cols in pieces:
+                picked = offsets[:, cols.start // 16 : cols.stop // 16]
                 nc.vector.tensor_tensor(
                     least[:, cols], values[b][:].indirect(picked), stream[b][:, cols], mybir.AluOpType.min
                 )
                 nc.scalar.activation(
                     gate[:, cols], gates[b][:].indirect(picked), mybir.ActivationFunctionType.Sigmoid
                 )
-            for j in range(0, N, PIECE):
-                cols = slice(j, j + PIECE)
+            for cols in pieces:
                 nc.vector.tensor_tensor(x[:, cols], least[:, cols], gate[:, cols], mybir.AluOpType.mult)
                 nc.sync.dma_start(out[rows, cols], x[:, cols])

@@ -2,10 +2,13 @@ import concourse.mybir as mybir
 
 P = 128
 PIECE = 256
-LAST_WIDTHS = (256, 256, 128, 128, 128, 128)
 LATE = 384
 F32 = mybir.dt.float32
 BYTES = 4 * (2 * 256 * 2048 + 2 * 256 * 1024) + 2 * 128 * 64
+
+
+def cut(start, stop):
+    return [slice(j, min(j + PIECE, stop)) for j in range(start, stop, PIECE)]
 
 
 def tile_lookup_vg_minsig_out_kernel(tc, tab, y, offs, out):
@@ -13,33 +16,27 @@ def tile_lookup_vg_minsig_out_kernel(tc, tab, y, offs, out):
     K, S = tab.shape[1], tab.shape[2]
     N = y.shape[1]
     BLOCKS = K // P
+    assert BLOCKS == 2
     with tc.tile_pool(name="held", bufs=1) as held, tc.tile_pool(name="blocks", bufs=BLOCKS) as blocks:
         offsets = held.tile([P, N // 16], mybir.dt.uint16)
+        values = [blocks.tile([P, S], F32, name="values") for b in range(BLOCKS)]
+        stream = [blocks.tile([P, N], F32, name="stream") for b in range(BLOCKS)]
+        gates = [blocks.tile([P, S], F32, name="gates") for b in range(BLOCKS)]
+        first, last = slice(0, P), slice(P, 2 * P)
 
-        warm_in = held.tile([P, 8], F32)
-        warm_out = held.tile([P, 8], F32)
-        nc.vector.memset(warm_in[:], 0.0)
-        nc.scalar.activation(warm_out[:], warm_in[:], mybir.ActivationFunctionType.Sigmoid)
+        nc.sync.dma_start(gates[0][:], tab[1, first, :])
+        nc.sync.dma_start(offsets[:], offs)
+        nc.sync.dma_start(values[0][:], tab[0, first, :])
+        for half in (slice(0, N // 2), slice(N // 2, N)):
+            nc.sync.dma_start(stream[0][:, half], y[first, half])
+        nc.sync.dma_start(values[1][:], tab[0, last, :])
+        nc.sync.dma_start(stream[1][:, : N - LATE], y[last, : N - LATE])
+        nc.sync.dma_start(gates[1][:], tab[1, last, :])
+        nc.sync.dma_start(stream[1][:, N - LATE :], y[last, N - LATE :])
 
-        values, stream, gates = [], [], []
-        for b in range(BLOCKS):
-            rows = slice(b * P, (b + 1) * P)
-            early = N - LATE if b == BLOCKS - 1 else N
-            values.append(blocks.tile([P, S], F32, name="values"))
-            nc.sync.dma_start(values[b][:], tab[0, rows, :])
-            if b == 0:
-                nc.sync.dma_start(offsets[:], offs)
-            stream.append(blocks.tile([P, N], F32, name="stream"))
-            nc.sync.dma_start(stream[b][:, :early], y[rows, :early])
-            gates.append(blocks.tile([P, S], F32, name="gates"))
-            nc.sync.dma_start(gates[b][:], tab[1, rows, :])
-            if early < N:
-                nc.sync.dma_start(stream[b][:, early:], y[rows, early:])
-
-        for b in range(BLOCKS):
-            rows = slice(b * P, (b + 1) * P)
-            widths = LAST_WIDTHS if b == BLOCKS - 1 else (PIECE,) * (N // PIECE)
-            pieces = [slice(sum(widths[:k]), sum(widths[: k + 1])) for k in range(len(widths))]
+        for b, rows in enumerate((first, last)):
+            edge = N - LATE if b == BLOCKS - 1 else N
+            pieces = cut(0, edge) + cut(edge, N)
             least = blocks.tile([P, N], F32)
             gate = blocks.tile([P, N], F32)
             x = blocks.tile([P, N], F32)

@@ -1,14 +1,15 @@
 import concourse.mybir as mybir
 
 P = 128
-PIECE = 256
+WIDE = 384
+NARROW = 256
 LATE = 384
 F32 = mybir.dt.float32
 BYTES = 4 * (2 * 256 * 2048 + 2 * 256 * 1024) + 2 * 128 * 64
 
 
-def cut(start, stop):
-    return [slice(j, min(j + PIECE, stop)) for j in range(start, stop, PIECE)]
+def cut(start, stop, width):
+    return [slice(j, min(j + width, stop)) for j in range(start, stop, width)]
 
 
 def tile_lookup_vg_minsig_out_kernel(tc, tab, y, offs, out):
@@ -36,7 +37,7 @@ def tile_lookup_vg_minsig_out_kernel(tc, tab, y, offs, out):
 
         for b, rows in enumerate((first, last)):
             edge = N - LATE if b == BLOCKS - 1 else N
-            pieces = cut(0, edge) + cut(edge, N)
+            pieces = cut(0, edge, WIDE) + cut(edge, N, NARROW)
             least = blocks.tile([P, N], F32)
             gate = blocks.tile([P, N], F32)
             x = blocks.tile([P, N], F32)

@@ -1,9 +1,9 @@
 import concourse.mybir as mybir
 
 P = 128
+LATE = 512
 WIDE = 384
 NARROW = 256
-LATE = 384
 F32 = mybir.dt.float32
 BYTES = 4 * (2 * 256 * 2048 + 2 * 256 * 1024) + 2 * 128 * 64
 
@@ -18,17 +18,17 @@ def tile_lookup_vg_minsig_out_kernel(tc, tab, y, offs, out):
     N = y.shape[1]
     BLOCKS = K // P
     assert BLOCKS == 2
+    first, last = slice(0, P), slice(P, 2 * P)
     with tc.tile_pool(name="held", bufs=1) as held, tc.tile_pool(name="blocks", bufs=BLOCKS) as blocks:
         offsets = held.tile([P, N // 16], mybir.dt.uint16)
         values = [blocks.tile([P, S], F32, name="values") for b in range(BLOCKS)]
         stream = [blocks.tile([P, N], F32, name="stream") for b in range(BLOCKS)]
         gates = [blocks.tile([P, S], F32, name="gates") for b in range(BLOCKS)]
-        first, last = slice(0, P), slice(P, 2 * P)
 
         nc.sync.dma_start(gates[0][:], tab[1, first, :])
         nc.sync.dma_start(offsets[:], offs)
         nc.sync.dma_start(values[0][:], tab[0, first, :])
-        for half in (slice(0, N // 2), slice(N // 2, N)):
+        for half in cut(0, N, N // 2):
             nc.sync.dma_start(stream[0][:, half], y[first, half])
         nc.sync.dma_start(values[1][:], tab[0, last, :])
         nc.sync.dma_start(stream[1][:, : N - LATE], y[last, : N - LATE])
@@ -36,16 +36,22 @@ def tile_lookup_vg_minsig_out_kernel(tc, tab, y, offs, out):
         nc.sync.dma_start(stream[1][:, N - LATE :], y[last, N - LATE :])
 
         for b, rows in enumerate((first, last)):
-            edge = N - LATE if b == BLOCKS - 1 else N
-            pieces = cut(0, edge, WIDE) + cut(edge, N, NARROW)
+            if b == BLOCKS - 1:
+                y_loads = cut(0, N, N - LATE)
+                pieces = cut(0, N - WIDE, WIDE) + cut(N - WIDE, N, NARROW)
+            else:
+                y_loads = cut(0, N, N // 2)
+                pieces = cut(0, N, WIDE)
             least = blocks.tile([P, N], F32)
             gate = blocks.tile([P, N], F32)
             x = blocks.tile([P, N], F32)
-            for cols in pieces:
+            for cols in y_loads:
                 picked = offsets[:, cols.start // 16 : cols.stop // 16]
                 nc.vector.tensor_tensor(
                     least[:, cols], values[b][:].indirect(picked), stream[b][:, cols], mybir.AluOpType.min
                 )
+            for cols in pieces:
+                picked = offsets[:, cols.start // 16 : cols.stop // 16]
                 nc.scalar.activation(
                     gate[:, cols], gates[b][:].indirect(picked), mybir.ActivationFunctionType.Sigmoid
                 )

@@ -1,9 +1,9 @@
 import concourse.mybir as mybir
 
 P = 128
-LATE = 512
 WIDE = 384
 NARROW = 256
+LATE = WIDE + NARROW
 F32 = mybir.dt.float32
 BYTES = 4 * (2 * 256 * 2048 + 2 * 256 * 1024) + 2 * 128 * 64
 
@@ -18,43 +18,62 @@ def tile_lookup_vg_minsig_out_kernel(tc, tab, y, offs, out):
     N = y.shape[1]
     BLOCKS = K // P
     assert BLOCKS == 2
-    first, last = slice(0, P), slice(P, 2 * P)
+    table = tab.rearrange("t (p b) s -> t b p s", b=BLOCKS)
+    both_y = y.rearrange("(p b) n -> p (b n)", b=BLOCKS)
+    result = out.rearrange("(p b) n -> b p n", b=BLOCKS)
+    early = BLOCKS * N - LATE
     with tc.tile_pool(name="held", bufs=1) as held, tc.tile_pool(name="blocks", bufs=BLOCKS) as blocks:
         offsets = held.tile([P, N // 16], mybir.dt.uint16)
+        stream = held.tile([P, BLOCKS * N], F32)
         values = [blocks.tile([P, S], F32, name="values") for b in range(BLOCKS)]
-        stream = [blocks.tile([P, N], F32, name="stream") for b in range(BLOCKS)]
         gates = [blocks.tile([P, S], F32, name="gates") for b in range(BLOCKS)]
+        least = [blocks.tile([P, N], F32, name="least") for b in range(BLOCKS)]
+        gate = [blocks.tile([P, N], F32, name="gate") for b in range(BLOCKS)]
+        x = [blocks.tile([P, N], F32, name="x") for b in range(BLOCKS)]
 
-        nc.sync.dma_start(gates[0][:], tab[1, first, :])
+        def picked(cols):
+            return offsets[:, cols.start // 16 : cols.stop // 16]
+
+        def load_y(start, stop):
+            nc.sync.dma_start(stream[:, start:stop], both_y[:, start:stop])
+
+        def minimum(b, cols):
+            block_y = stream[:, b * N + cols.start : b * N + cols.stop]
+            nc.vector.tensor_tensor(
+                least[b][:, cols], values[b][:].indirect(picked(cols)), block_y, mybir.AluOpType.min
+            )
+
+        def sigmoid(b, cols):
+            nc.scalar.activation(
+                gate[b][:, cols], gates[b][:].indirect(picked(cols)), mybir.ActivationFunctionType.Sigmoid
+            )
+
+        def product(b, cols):
+            nc.vector.tensor_tensor(x[b][:, cols], least[b][:, cols], gate[b][:, cols], mybir.AluOpType.mult)
+            nc.sync.dma_start(result[b][:, cols], x[b][:, cols])
+
+        nc.sync.dma_start(gates[0][:], table[1, 0])
         nc.sync.dma_start(offsets[:], offs)
-        nc.sync.dma_start(values[0][:], tab[0, first, :])
-        for half in cut(0, N, N // 2):
-            nc.sync.dma_start(stream[0][:, half], y[first, half])
-        nc.sync.dma_start(values[1][:], tab[0, last, :])
-        nc.sync.dma_start(stream[1][:, : N - LATE], y[last, : N - LATE])
-        nc.sync.dma_start(gates[1][:], tab[1, last, :])
-        nc.sync.dma_start(stream[1][:, N - LATE :], y[last, N - LATE :])
+        nc.sync.dma_start(values[0][:], table[0, 0])
+        load_y(0, N // 2)
+        load_y(N // 2, early)
+        nc.sync.dma_start(values[1][:], table[0, 1])
+        nc.sync.dma_start(gates[1][:], table[1, 1])
+        load_y(early, early + WIDE)
+        load_y(early + WIDE, BLOCKS * N)
 
-        for b, rows in enumerate((first, last)):
-            if b == BLOCKS - 1:
-                y_loads = cut(0, N, N - LATE)
-                pieces = cut(0, N - WIDE, WIDE) + cut(N - WIDE, N, NARROW)
-            else:
-                y_loads = cut(0, N, N // 2)
-                pieces = cut(0, N, WIDE)
-            least = blocks.tile([P, N], F32)
-            gate = blocks.tile([P, N], F32)
-            x = blocks.tile([P, N], F32)
-            for cols in y_loads:
-                picked = offsets[:, cols.start // 16 : cols.stop // 16]
-                nc.vector.tensor_tensor(
-                    least[:, cols], values[b][:].indirect(picked), stream[b][:, cols], mybir.AluOpType.min
-                )
-            for cols in pieces:
-                picked = offsets[:, cols.start // 16 : cols.stop // 16]
-                nc.scalar.activation(
-                    gate[:, cols], gates[b][:].indirect(picked), mybir.ActivationFunctionType.Sigmoid
-                )
-            for cols in pieces:
-                nc.vector.tensor_tensor(x[:, cols], least[:, cols], gate[:, cols], mybir.AluOpType.mult)
-                nc.sync.dma_start(out[rows, cols], x[:, cols])
+        for cols in cut(0, N, N // 2):
+            minimum(0, cols)
+        for cols in cut(0, N, WIDE):
+            sigmoid(0, cols)
+            product(0, cols)
+
+        first = slice(0, N - LATE)
+        minimum(1, first)
+        minimum(1, slice(N - LATE, N - NARROW))
+        sigmoid(1, first)
+        product(1, first)
+        minimum(1, slice(N - NARROW, N))
+        for cols in cut(N - LATE, N, NARROW):
+            sigmoid(1, cols)
+            product(1, cols)

@@ -2,8 +2,8 @@ import concourse.mybir as mybir
 
 P = 128
 WIDE = 384
-NARROW = 256
-LATE = WIDE + NARROW
+STEP = 64
+LATE = 576
 F32 = mybir.dt.float32
 BYTES = 4 * (2 * 256 * 2048 + 2 * 256 * 1024) + 2 * 128 * 64
 
@@ -64,16 +64,17 @@ def tile_lookup_vg_minsig_out_kernel(tc, tab, y, offs, out):
 
         for cols in cut(0, N, N // 2):
             minimum(0, cols)
-        for cols in cut(0, N, WIDE):
+        for cols in cut(0, N, N // 2):
             sigmoid(0, cols)
             product(0, cols)
 
-        first = slice(0, N - LATE)
-        minimum(1, first)
-        minimum(1, slice(N - LATE, N - NARROW))
-        sigmoid(1, first)
-        product(1, first)
-        minimum(1, slice(N - NARROW, N))
-        for cols in cut(N - LATE, N, NARROW):
+        edges = [0, WIDE] + [N - STEP * k * (k + 1) // 2 for k in (3, 2, 1, 0)]
+        pieces = [slice(a, b) for a, b in zip(edges, edges[1:])]
+        minimum(1, slice(0, N - LATE))
+        minimum(1, slice(N - LATE, N - LATE + WIDE))
+        sigmoid(1, pieces[0])
+        product(1, pieces[0])
+        minimum(1, slice(N - LATE + WIDE, N))
+        for cols in pieces[1:]:
             sigmoid(1, cols)
             product(1, cols)

@@ -52,9 +52,9 @@ def tile_lookup_vg_minsig_out_kernel(tc, tab, y, offs, out):
             nc.vector.tensor_tensor(x[b][:, cols], least[b][:, cols], gate[b][:, cols], mybir.AluOpType.mult)
             nc.sync.dma_start(result[b][:, cols], x[b][:, cols])
 
+        nc.sync.dma_start(values[0][:], table[0, 0])
         nc.sync.dma_start(gates[0][:], table[1, 0])
         nc.sync.dma_start(offsets[:], offs)
-        nc.sync.dma_start(values[0][:], table[0, 0])
         load_y(0, N // 2)
         load_y(N // 2, early)
         nc.sync.dma_start(values[1][:], table[0, 1])

@@ -50,7 +50,9 @@ def tile_lookup_vg_minsig_out_kernel(tc, tab, y, offs, out):
 
         def product(b, cols):
             nc.vector.tensor_tensor(x[b][:, cols], least[b][:, cols], gate[b][:, cols], mybir.AluOpType.mult)
-            nc.sync.dma_start(result[b][:, cols], x[b][:, cols])
+
+        def store(b, cols, queue=nc.sync):
+            queue.dma_start(result[b][:, cols], x[b][:, cols])
 
         nc.sync.dma_start(values[0][:], table[0, 0])
         nc.sync.dma_start(gates[0][:], table[1, 0])
@@ -67,6 +69,7 @@ def tile_lookup_vg_minsig_out_kernel(tc, tab, y, offs, out):
         for cols in cut(0, N, N // 2):
             sigmoid(0, cols)
             product(0, cols)
+            store(0, cols, nc.scalar if cols.stop == N else nc.sync)
 
         edges = [0, WIDE] + [N - STEP * k * (k + 1) // 2 for k in (3, 2, 1, 0)]
         pieces = [slice(a, b) for a, b in zip(edges, edges[1:])]
@@ -74,7 +77,9 @@ def tile_lookup_vg_minsig_out_kernel(tc, tab, y, offs, out):
         minimum(1, slice(N - LATE, N - LATE + WIDE))
         sigmoid(1, pieces[0])
         product(1, pieces[0])
+        store(1, pieces[0])
         minimum(1, slice(N - LATE + WIDE, N))
         for cols in pieces[1:]:
             sigmoid(1, cols)
             product(1, cols)
+            store(1, cols, nc.scalar if cols == pieces[-2] else nc.sync)

@@ -1,35 +1,33 @@
 import concourse.mybir as mybir
 
 P = 128
-WIDE = 384
-STEP = 64
-LATE = 576
+PIECES = (448, 192, 192, 128, 64)
+LATE = (384, 192)
 F32 = mybir.dt.float32
 BYTES = 4 * (2 * 256 * 2048 + 2 * 256 * 1024) + 2 * 128 * 64
 
 
-def cut(start, stop, width):
-    return [slice(j, min(j + width, stop)) for j in range(start, stop, width)]
+def lay(start, widths):
+    edges = [start + sum(widths[:k]) for k in range(len(widths) + 1)]
+    return [slice(a, b) for a, b in zip(edges, edges[1:])]
 
 
 def tile_lookup_vg_minsig_out_kernel(tc, tab, y, offs, out):
     nc = tc.nc
-    K, S = tab.shape[1], tab.shape[2]
-    N = y.shape[1]
-    BLOCKS = K // P
-    assert BLOCKS == 2
-    table = tab.rearrange("t (p b) s -> t b p s", b=BLOCKS)
-    both_y = y.rearrange("(p b) n -> p (b n)", b=BLOCKS)
-    result = out.rearrange("(p b) n -> b p n", b=BLOCKS)
-    early = BLOCKS * N - LATE
-    with tc.tile_pool(name="held", bufs=1) as held, tc.tile_pool(name="blocks", bufs=BLOCKS) as blocks:
+    S, N = tab.shape[2], y.shape[1]
+    assert tab.shape[1] == 2 * P and sum(PIECES) == N
+    table = tab.rearrange("t (p b) s -> t b p s", b=2)
+    both_y = y.rearrange("(p b) n -> p (b n)", b=2)
+    result = out.rearrange("(p b) n -> b p n", b=2)
+    early = N - sum(LATE)
+    with tc.tile_pool(name="held", bufs=1) as held, tc.tile_pool(name="blocks", bufs=2) as blocks:
         offsets = held.tile([P, N // 16], mybir.dt.uint16)
-        stream = held.tile([P, BLOCKS * N], F32)
-        values = [blocks.tile([P, S], F32, name="values") for b in range(BLOCKS)]
-        gates = [blocks.tile([P, S], F32, name="gates") for b in range(BLOCKS)]
-        least = [blocks.tile([P, N], F32, name="least") for b in range(BLOCKS)]
-        gate = [blocks.tile([P, N], F32, name="gate") for b in range(BLOCKS)]
-        x = [blocks.tile([P, N], F32, name="x") for b in range(BLOCKS)]
+        stream = held.tile([P, 2 * N], F32)
+        values = [blocks.tile([P, S], F32, name="values") for b in range(2)]
+        gates = [blocks.tile([P, S], F32, name="gates") for b in range(2)]
+        least = [blocks.tile([P, N], F32, name="least") for b in range(2)]
+        gate = [blocks.tile([P, N], F32, name="gate") for b in range(2)]
+        x = [blocks.tile([P, N], F32, name="x") for b in range(2)]
 
         def picked(cols):
             return offsets[:, cols.start // 16 : cols.stop // 16]
@@ -51,35 +49,35 @@ def tile_lookup_vg_minsig_out_kernel(tc, tab, y, offs, out):
         def product(b, cols):
             nc.vector.tensor_tensor(x[b][:, cols], least[b][:, cols], gate[b][:, cols], mybir.AluOpType.mult)
 
-        def store(b, cols, queue=nc.sync):
+        def store(b, cols, queue):
             queue.dma_start(result[b][:, cols], x[b][:, cols])
+
+        halves = lay(0, (N // 2, N // 2))
+        pieces = lay(0, PIECES)
+        late = lay(early, LATE)
 
         nc.sync.dma_start(values[0][:], table[0, 0])
         nc.sync.dma_start(gates[0][:], table[1, 0])
         nc.sync.dma_start(offsets[:], offs)
         load_y(0, N // 2)
-        load_y(N // 2, early)
+        load_y(N // 2, N + early)
         nc.sync.dma_start(values[1][:], table[0, 1])
         nc.sync.dma_start(gates[1][:], table[1, 1])
-        load_y(early, early + WIDE)
-        load_y(early + WIDE, BLOCKS * N)
+        for cols in late:
+            load_y(N + cols.start, N + cols.stop)
 
-        for cols in cut(0, N, N // 2):
+        for cols in halves:
             minimum(0, cols)
-        for cols in cut(0, N, N // 2):
+        for cols, queue in zip(halves, (nc.sync, nc.scalar)):
             sigmoid(0, cols)
             product(0, cols)
-            store(0, cols, nc.scalar if cols.stop == N else nc.sync)
+            store(0, cols, queue)
 
-        edges = [0, WIDE] + [N - STEP * k * (k + 1) // 2 for k in (3, 2, 1, 0)]
-        pieces = [slice(a, b) for a, b in zip(edges, edges[1:])]
-        minimum(1, slice(0, N - LATE))
-        minimum(1, slice(N - LATE, N - LATE + WIDE))
-        sigmoid(1, pieces[0])
-        product(1, pieces[0])
-        store(1, pieces[0])
-        minimum(1, slice(N - LATE + WIDE, N))
-        for cols in pieces[1:]:
+        minimum(1, slice(0, early))
+        minimum(1, late[0])
+        for cols in pieces:
+            if cols == pieces[1]:
+                minimum(1, late[1])
             sigmoid(1, cols)
             product(1, cols)
             store(1, cols, nc.scalar if cols == pieces[-2] else nc.sync)

@@ -74,10 +74,11 @@ def tile_lookup_vg_minsig_out_kernel(tc, tab, y, offs, out):
             store(0, cols, queue)
 
         minimum(1, slice(0, early))
+        for cols in (pieces[0], slice(pieces[1].start, pieces[2].stop), *pieces[3:]):
+            sigmoid(1, cols)
         minimum(1, late[0])
         for cols in pieces:
             if cols == pieces[1]:
                 minimum(1, late[1])
-            sigmoid(1, cols)
             product(1, cols)
             store(1, cols, nc.scalar if cols == pieces[-2] else nc.sync)

import concourse.mybir as mybir

P = 128
PIECES = (448, 192, 192, 128, 64)
LATE = (384, 192)
F32 = mybir.dt.float32
BYTES = 4 * (2 * 256 * 2048 + 2 * 256 * 1024) + 2 * 128 * 64


def lay(start, widths):
    edges = [start + sum(widths[:k]) for k in range(len(widths) + 1)]
    return [slice(a, b) for a, b in zip(edges, edges[1:])]


def tile_lookup_vg_minsig_out_kernel(tc, tab, y, offs, out):
    nc = tc.nc
    S, N = tab.shape[2], y.shape[1]
    assert tab.shape[1] == 2 * P and sum(PIECES) == N
    table = tab.rearrange("t (p b) s -> t b p s", b=2)
    both_y = y.rearrange("(p b) n -> p (b n)", b=2)
    result = out.rearrange("(p b) n -> b p n", b=2)
    early = N - sum(LATE)
    with tc.tile_pool(name="held", bufs=1) as held, tc.tile_pool(name="blocks", bufs=2) as blocks:
        offsets = held.tile([P, N // 16], mybir.dt.uint16)
        stream = held.tile([P, 2 * N], F32)
        values = [blocks.tile([P, S], F32, name="values") for b in range(2)]
        gates = [blocks.tile([P, S], F32, name="gates") for b in range(2)]
        least = [blocks.tile([P, N], F32, name="least") for b in range(2)]
        gate = [blocks.tile([P, N], F32, name="gate") for b in range(2)]
        x = [blocks.tile([P, N], F32, name="x") for b in range(2)]

        def picked(cols):
            return offsets[:, cols.start // 16 : cols.stop // 16]

        def load_y(start, stop):
            nc.sync.dma_start(stream[:, start:stop], both_y[:, start:stop])

        def minimum(b, cols):
            block_y = stream[:, b * N + cols.start : b * N + cols.stop]
            nc.vector.tensor_tensor(
                least[b][:, cols], values[b][:].indirect(picked(cols)), block_y, mybir.AluOpType.min
            )

        def sigmoid(b, cols):
            nc.scalar.activation(
                gate[b][:, cols], gates[b][:].indirect(picked(cols)), mybir.ActivationFunctionType.Sigmoid
            )

        def product(b, cols):
            nc.vector.tensor_tensor(x[b][:, cols], least[b][:, cols], gate[b][:, cols], mybir.AluOpType.mult)

        def store(b, cols, queue):
            queue.dma_start(result[b][:, cols], x[b][:, cols])

        halves = lay(0, (N // 2, N // 2))
        pieces = lay(0, PIECES)
        late = lay(early, LATE)

        nc.sync.dma_start(values[0][:], table[0, 0])
        nc.sync.dma_start(gates[0][:], table[1, 0])
        nc.sync.dma_start(offsets[:], offs)
        load_y(0, N // 2)
        load_y(N // 2, N + early)
        nc.sync.dma_start(values[1][:], table[0, 1])
        nc.sync.dma_start(gates[1][:], table[1, 1])
        for cols in late:
            load_y(N + cols.start, N + cols.stop)

        for cols in halves:
            minimum(0, cols)
        for cols, queue in zip(halves, (nc.sync, nc.scalar)):
            sigmoid(0, cols)
            product(0, cols)
            store(0, cols, queue)

        minimum(1, slice(0, early))
        for cols in (pieces[0], slice(pieces[1].start, pieces[2].stop), *pieces[3:]):
            sigmoid(1, cols)
        minimum(1, late[0])
        for cols in pieces:
            if cols == pieces[1]:
                minimum(1, late[1])
            product(1, cols)
            store(1, cols, nc.scalar if cols == pieces[-2] else nc.sync)
